import numpy as np
import ml_dtypes


def mxq(x, axis, fmt="e4m3"):
    dtype, down = {"e4m3": (ml_dtypes.float8_e4m3fn, 7), "e5m2": (ml_dtypes.float8_e5m2, 14)}[fmt]
    v = np.moveaxis(np.asarray(x, np.float32).astype(ml_dtypes.bfloat16).astype(np.float64), axis, -1)
    blocks = v.reshape(v.shape[:-1] + (-1, 32))
    amax = np.abs(blocks).max(-1, keepdims=True)
    byte = np.maximum(np.where(amax > 0, np.frexp(amax)[1] - 1 + 127, 0) - down, 1)
    scale = np.exp2(byte - 127.0)
    codes = (blocks / scale).astype(np.float32).astype(dtype).astype(np.float64)
    return np.moveaxis((codes * scale).reshape(v.shape), -1, axis)


WIDE = False


def mx_kscale(k):
    if not WIDE:
        return np.ones(k)
    levels = np.array([10, -10, 5, -5, 0])
    if k % 512:
        return np.exp2(np.random.permutation(np.resize(levels, k // 32))).repeat(32)
    a = np.empty((k // 512, 16))
    for p in range(k // 512):
        a[p, :8] = np.random.permutation(np.resize(levels, 8))
        for g in range(8):
            far = levels[np.abs(levels - a[p, g]) >= 10]
            a[p, g + 8] = far[np.random.randint(len(far))]
    return np.exp2(a.ravel()).repeat(32)


def f64(x):
    return np.asarray(x).astype(np.float64)


def striped(idx):
    return np.tile(idx.reshape(-1, 16).T, (8, 1)).astype(np.uint16)


def unstriped(offs):
    return offs[:16].T.reshape(-1).astype(np.int64)


def pack_weight(w):
    k, n = w.shape
    w = f64(np.asarray(w, np.float32).astype(ml_dtypes.bfloat16)).reshape(k // 32, 32, n)
    amax = np.abs(w).max(1)
    byte = np.clip(np.where(amax > 0, np.frexp(amax)[1] - 1 + 127 - 7, 1), 1, 254)
    scaled = (w * np.exp2(127.0 - byte)[:, None, :]).reshape(k, n).astype(np.float32)
    words = np.ascontiguousarray(scaled.reshape(k // 512, 128, 4, n).transpose(0, 1, 3, 2)).astype(ml_dtypes.float8_e4m3fn).view(np.uint8)
    return words, np.ascontiguousarray(byte.astype(np.uint8).reshape(k // 512, 16, n))


def unpack_weight(words, scales):
    g, p, n, _ = words.shape
    vals = np.ascontiguousarray(words).view(ml_dtypes.float8_e4m3fn).astype(np.float64) * np.repeat(np.exp2(scales.astype(np.float64) - 127.0), 8, axis=1)[..., None]
    return vals.transpose(0, 1, 3, 2).reshape(g * 512, n)


K, T, S, V, N = 1024, 2048, 1024, 512, 256
P = 2 ** 7


def setup_inputs():
    n = np.random.standard_normal
    s = mx_kscale(K)[:, None]
    packed_xT = pack_weight(n((K, T)) * s)
    return {
        "x_words": packed_xT[0],
        "x_scales": packed_xT[1],
        "w1": (n((K, N)) / np.sqrt(K) / s).astype(np.float32),
        "bound": np.tile(np.random.uniform(0.3, 1.2, V), (P, 1)).astype(np.float32),
        "offs": striped(np.random.permutation(T)[:S]),
        "cen": striped(np.random.permutation(S)[:V]),
        "pos1": striped(np.random.permutation(S)[:V]),
        "pos2": striped(np.random.permutation(S)[:V]),
        "pos3": striped(np.random.permutation(S)[:V]),
    }


def reference(x_words, x_scales, w1, bound, offs, cen, pos1, pos2, pos3):
    xq = unpack_weight(x_words, x_scales)[:, unstriped(offs)]
    y = mxq(f64(w1), 0, "e4m3").T @ xq
    yc = y[:, unstriped(cen)]
    low = -1.0 * f64(bound)[:1]
    return yc + (np.maximum(np.minimum(y[:, unstriped(pos1)] - yc, f64(bound)[:1]), low) + np.maximum(np.minimum(y[:, unstriped(pos2)] - yc, f64(bound)[:1]), low) + np.maximum(np.minimum(y[:, unstriped(pos3)] - yc, f64(bound)[:1]), low)) / 3

@@ -1,0 +1,208 @@
+from contextlib import ExitStack
+
+import concourse.mybir as mybir
+from concourse.masks import make_identity
+
+K, T, S, V, N = 1024, 2048, 1024, 512, 256
+FLOPS = 2 * K * S * N
+
+F32 = mybir.dt.float32
+BF16 = mybir.dt.bfloat16
+I32 = mybir.dt.int32
+U32 = mybir.dt.uint32
+U16 = mybir.dt.uint16
+U8 = mybir.dt.uint8
+FP8X4 = mybir.dt.float8_e4m3fn_x4
+ALU = mybir.AluOpType
+
+P = 128
+PACK = 4
+PASSES = K // (P * PACK)
+BLOCKS = N // P
+LANES = 16
+NEIGHBOURS = 3
+UNITS = [(0, 0, 256, (6, 7), 2), (0, 256, 256, (0, 1), 3), (1, 0, 256, (4, 5), 2), (1, 256, 128, (6,), 3), (1, 384, 128, (7,), 0)]
+
+
+def tile_picked_huber_none_p_kernel(
+    tc, x_words, x_scales, w1, bound, offs, cen, pos1, pos2, pos3, out
+):
+    nc = tc.nc
+    with ExitStack() as ctx:
+        keep = ctx.enter_context(tc.tile_pool(name="keep", bufs=1))
+        psum = ctx.enter_context(tc.psum_pool(name="psum", bufs=1))
+
+        def load_list(name, src):
+            tile = keep.tile(list(src.shape), U16, name=name)
+            nc.sync.dma_start(tile[:], src)
+            return tile
+
+        scale_win = keep.tile([P, T], U8, name="scale_win", align_bytes=64)
+        nc.vector.memset(scale_win[:].bitcast(I32), 0)
+        offs_sb = load_list("offs_sb", offs)
+        for q in range(4):
+            nc.sync.dma_start(
+                scale_win[32 * q : 32 * q + 4 * PASSES, :].bitcast(I32),
+                x_scales[:, 4 * q : 4 * q + 4, :].bitcast(I32),
+            )
+        word_win, w_raw = [], {}
+
+        def load_weights(z, b):
+            raw = keep.tile([P, PACK, P], F32, name="w_raw%d%d" % (z, b))
+            rows = w1[z * P * PACK : (z + 1) * P * PACK, b * P : (b + 1) * P]
+            nc.sync.dma_start(raw[:], rows.rearrange("(p j) c -> p j c", j=PACK))
+            w_raw[z, b] = raw
+
+        for z in range(PASSES):
+            win = keep.tile([P, T], I32, name="word_win%d" % z, align_bytes=64)
+            nc.sync.dma_start(win[:], x_words[z].rearrange("p n t -> p (n t)").bitcast(I32))
+            word_win.append(win)
+            load_weights(z, 0)
+        for z in range(PASSES):
+            load_weights(z, 1)
+        cen_sb = load_list("cen_sb", cen)
+        pos_sb = [load_list("pos%d_sb" % d, src) for d, src in enumerate((pos1, pos2, pos3))]
+        hi = keep.tile([P, V // P], F32, name="hi")
+        with nc.allow_non_contiguous_dma(reason="one bound a partition"):
+            nc.sync.dma_start(hi[:], bound[0, :].rearrange("(c p) -> p c", p=P))
+        lo = keep.tile([P, V // P], F32, name="lo")
+        nc.scalar.mul(lo[:], hi[:], -1.0)
+
+        ident = keep.tile([P, P], F32, name="ident")
+        make_identity(nc, ident[:])
+
+        def entries(tile, start, count):
+            return tile[:, start // LANES : (start + count) // LANES]
+
+        x_sc = keep.tile([P, S], U8, name="x_sc", align_bytes=64)
+        nc.vector.tensor_copy(x_sc[:], scale_win[:].indirect(offs_sb[:]))
+        pieces = [(0, 512), (512, 256), (768, 256)]
+        x_codes = {}
+
+        def gather_words(z, start, count, tag):
+            codes = keep.tile([P, count], U32, name="x_codes", tag=tag, align_bytes=64)
+            nc.vector.tensor_copy(codes[:], word_win[z][:].bitcast(U32).indirect(entries(offs_sb, start, count)))
+            return codes
+
+        w_codes, w_sc = {}, {}
+
+        def quantise_weights(z, b):
+            grouped = keep.tile([P, P, PACK], BF16, name="w_bf", tag="w_bf%d%d" % (z, b), align_bytes=64)
+            nc.scalar.copy(
+                grouped[:].rearrange("p (c i) j -> p c j i", i=4),
+                w_raw[z, b][:].rearrange("p j (c i) -> p c j i", i=4),
+            )
+            w_codes[z, b] = keep.tile([P, P], U32, name="w_codes%d%d" % (z, b), align_bytes=64)
+            w_sc[z, b] = keep.tile([P, P], U8, name="w_sc%d%d" % (z, b), align_bytes=64)
+            nc.vector.quantize_mx(
+                out=w_codes[z, b][:].bitcast(FP8X4),
+                scales=w_sc[z, b][:],
+                in_=grouped[:].rearrange("p c j -> p (c j)"),
+            )
+
+        def bank(index, shape):
+            return psum.tile(shape, F32, name="bank", tag="bank%d" % index)
+
+        def project(b, piece, bank_index):
+            start, count = piece
+            cols = slice(start, start + count)
+            acc = bank(bank_index, [P, count])
+            for z in range(PASSES):
+                nc.tensor.matmul_mx(
+                    out=acc[:],
+                    lhsT=w_codes[z, b][:].bitcast(FP8X4),
+                    lhsT_scale=w_sc[z, b][:],
+                    rhs=x_codes[z, start].bitcast(FP8X4),
+                    rhs_scale=x_sc[4 * z :, cols],
+                    start=(z == 0),
+                    stop=(z == PASSES - 1),
+                )
+            nc.scalar.copy(y[b][:, cols], acc[:])
+
+        y = [keep.tile([P, S], F32, name="y%d" % b) for b in range(BLOCKS)]
+        first = gather_words(0, 0, S, "x_first")
+        for start, count in pieces:
+            x_codes[0, start] = first[:, start : start + count]
+        quantise_weights(0, 0)
+        x_codes[1, 0] = gather_words(1, 0, 512, "x_second")[:]
+        quantise_weights(1, 0)
+        x_codes[1, 512] = gather_words(1, 512, 256, "w_bf10")[:]
+        x_codes[1, 768] = gather_words(1, 768, 256, "x_last")[:]
+        for i, piece in enumerate(pieces):
+            project(0, piece, i)
+        for z in range(PASSES):
+            quantise_weights(z, 1)
+        for i, piece in enumerate(pieces):
+            project(1, piece, 3 + i)
+
+        last = len(UNITS) - 1
+
+        def work(k, role, shape, tag=None):
+            return keep.tile(shape, F32, name=role, tag=tag or "%s%d" % (role, k))
+
+        def gather_centres(k):
+            b, v0, width = UNITS[k][:3]
+            yc = work(k, "yc", [P, width])
+            nc.vector.tensor_copy(yc[:], y[b][:].indirect(entries(cen_sb, v0, width)))
+            neg = work(k, "neg", [P, width])
+            nc.scalar.mul(neg[:], yc[:], -1.0)
+            pulls = [bank(index, [P, NEIGHBOURS, P]) for index in UNITS[k][3]]
+            return yc, neg, pulls
+
+        def gather_neighbours(k, d, tag):
+            b, v0, width = UNITS[k][:3]
+            yc, neg, pulls = centres[k]
+            yp = work(k, "yp%d" % d, [P, width], tag)
+            nc.vector.tensor_copy(yp[:], y[b][:].indirect(entries(pos_sb[d], v0, width)))
+            for c, pull in enumerate(pulls):
+                cols = slice(c * P, (c + 1) * P)
+                nc.tensor.matmul(pull[:, d, :], neg[:, cols], ident[:], start=True, stop=False, is_transpose=True)
+                nc.tensor.matmul(pull[:, d, :], yp[:, cols], ident[:], start=False, stop=True, is_transpose=True)
+
+        def clip_and_turn_back(k):
+            v0, pulls = UNITS[k][1], centres[k][2]
+            total = bank(UNITS[k][4], [P, len(pulls) * P])
+            for c, pull in enumerate(pulls):
+                chunk = v0 // P + c
+                clipped = work(k, "clipped%d" % c, [P, NEIGHBOURS, P])
+                if k == last:
+                    nc.vector.tensor_scalar(
+                        clipped[:], pull[:], hi[:, chunk : chunk + 1], lo[:, chunk : chunk + 1], ALU.min, ALU.max
+                    )
+                else:
+                    staged = work(k, "staged%d" % c, [P, NEIGHBOURS, P])
+                    nc.scalar.copy(staged[:], pull[:])
+                    nc.gpsimd.tensor_scalar(
+                        clipped[:], staged[:], hi[:, chunk : chunk + 1], lo[:, chunk : chunk + 1], ALU.min, ALU.max
+                    )
+                for d in range(NEIGHBOURS):
+                    nc.tensor.matmul(
+                        total[:, c * P : (c + 1) * P],
+                        clipped[:, d, :],
+                        ident[:],
+                        start=(d == 0),
+                        stop=(d == NEIGHBOURS - 1),
+                        is_transpose=True,
+                    )
+            return total
+
+        def finish(k):
+            b, v0, width = UNITS[k][:3]
+            result = work(k, "result", [P, width])
+            nc.vector.scalar_tensor_tensor(result[:], summed[k][:], 1.0 / NEIGHBOURS, centres[k][0][:], ALU.mult, ALU.add)
+            nc.sync.dma_start(out[b * P : (b + 1) * P, v0 : v0 + width], result[:])
+
+        centres, summed = {}, {}
+        for k in range(len(UNITS)):
+            centres[k] = gather_centres(k)
+            for d in range(NEIGHBOURS):
+                tag = None
+                if d == 0 and k >= 2:
+                    finish(k - 2)
+                if d == 0 and k >= 1:
+                    summed[k - 1] = clip_and_turn_back(k - 1)
+                    pass
+                gather_neighbours(k, d, tag)
+        finish(last - 1)
+        summed[last] = clip_and_turn_back(last)
+        finish(last)

@@ -21,7 +21,11 @@ PASSES = K // (P * PACK)
 BLOCKS = N // P
 LANES = 16
 NEIGHBOURS = 3
-UNITS = [(0, 0, 256, (6, 7), 2), (0, 256, 256, (0, 1), 3), (1, 0, 256, (4, 5), 2), (1, 256, 128, (6,), 3), (1, 384, 128, (7,), 0)]
+CHUNKS = BLOCKS * V // P
+PULL_BANKS = (6, 7, 0, 1)
+LAG = 3
+DIRECT = 2
+FINISHES = [(0, 2, 2, "staged1"), (2, 2, 3, "staged3"), (4, 2, 4, None), (6, 1, 5, None), (7, 1, 2, None)]
 
 
 def tile_picked_huber_none_p_kernel(
@@ -40,17 +44,20 @@ def tile_picked_huber_none_p_kernel(
         scale_win = keep.tile([P, T], U8, name="scale_win", align_bytes=64)
         nc.vector.memset(scale_win[:].bitcast(I32), 0)
         offs_sb = load_list("offs_sb", offs)
+        cen_sb = load_list("cen_sb", cen)
+        pos_sb = [load_list("pos%d_sb" % d, (pos1, pos2, pos3)[d]) for d in range(1)]
         for q in range(4):
             nc.sync.dma_start(
                 scale_win[32 * q : 32 * q + 4 * PASSES, :].bitcast(I32),
                 x_scales[:, 4 * q : 4 * q + 4, :].bitcast(I32),
             )
         word_win, w_raw = [], {}
+        y = [keep.tile([P, 2 * S], F32, name="y%d" % b) for b in range(BLOCKS)]
 
         def load_weights(z, b):
-            raw = keep.tile([P, PACK, P], F32, name="w_raw%d%d" % (z, b))
+            raw = y[b][:, S + z * PACK * P : S + (z + 1) * PACK * P].rearrange("p (j c) -> p j c", j=PACK)
             rows = w1[z * P * PACK : (z + 1) * P * PACK, b * P : (b + 1) * P]
-            nc.sync.dma_start(raw[:], rows.rearrange("(p j) c -> p j c", j=PACK))
+            nc.sync.dma_start(raw, rows.rearrange("(p j) c -> p j c", j=PACK))
             w_raw[z, b] = raw
 
         for z in range(PASSES):
@@ -60,8 +67,7 @@ def tile_picked_huber_none_p_kernel(
             load_weights(z, 0)
         for z in range(PASSES):
             load_weights(z, 1)
-        cen_sb = load_list("cen_sb", cen)
-        pos_sb = [load_list("pos%d_sb" % d, src) for d, src in enumerate((pos1, pos2, pos3))]
+        pos_sb = pos_sb + [load_list("pos%d_sb" % d, (pos1, pos2, pos3)[d]) for d in range(1, 3)]
         hi = keep.tile([P, V // P], F32, name="hi")
         with nc.allow_non_contiguous_dma(reason="one bound a partition"):
             nc.sync.dma_start(hi[:], bound[0, :].rearrange("(c p) -> p c", p=P))
@@ -90,7 +96,7 @@ def tile_picked_huber_none_p_kernel(
             grouped = keep.tile([P, P, PACK], BF16, name="w_bf", tag="w_bf%d%d" % (z, b), align_bytes=64)
             nc.scalar.copy(
                 grouped[:].rearrange("p (c i) j -> p c j i", i=4),
-                w_raw[z, b][:].rearrange("p j (c i) -> p c j i", i=4),
+                w_raw[z, b].rearrange("p j (c i) -> p c j i", i=4),
             )
             w_codes[z, b] = keep.tile([P, P], U32, name="w_codes%d%d" % (z, b), align_bytes=64)
             w_sc[z, b] = keep.tile([P, P], U8, name="w_sc%d%d" % (z, b), align_bytes=64)
@@ -119,7 +125,6 @@ def tile_picked_huber_none_p_kernel(
                 )
             nc.scalar.copy(y[b][:, cols], acc[:])
 
-        y = [keep.tile([P, S], F32, name="y%d" % b) for b in range(BLOCKS)]
         first = gather_words(0, 0, S, "x_first")
         for start, count in pieces:
             x_codes[0, start] = first[:, start : start + count]
@@ -135,74 +140,58 @@ def tile_picked_huber_none_p_kernel(
         for i, piece in enumerate(pieces):
             project(1, piece, 3 + i)
 
-        last = len(UNITS) - 1
-
         def work(k, role, shape, tag=None):
             return keep.tile(shape, F32, name=role, tag=tag or "%s%d" % (role, k))
 
-        def gather_centres(k):
-            b, v0, width = UNITS[k][:3]
-            yc = work(k, "yc", [P, width])
-            nc.vector.tensor_copy(yc[:], y[b][:].indirect(entries(cen_sb, v0, width)))
-            neg = work(k, "neg", [P, width])
-            nc.scalar.mul(neg[:], yc[:], -1.0)
-            pulls = [bank(index, [P, NEIGHBOURS, P]) for index in UNITS[k][3]]
-            return yc, neg, pulls
+        def gather_centres(b):
+            neg = work(b, "neg", [P, V])
+            nc.vector.tensor_scalar(neg[:], y[b][:].indirect(cen_sb[:]), -1.0, 0.0, ALU.mult, ALU.add)
+            return neg
 
-        def gather_neighbours(k, d, tag):
-            b, v0, width = UNITS[k][:3]
-            yc, neg, pulls = centres[k]
-            yp = work(k, "yp%d" % d, [P, width], tag)
-            nc.vector.tensor_copy(yp[:], y[b][:].indirect(entries(pos_sb[d], v0, width)))
-            for c, pull in enumerate(pulls):
-                cols = slice(c * P, (c + 1) * P)
-                nc.tensor.matmul(pull[:, d, :], neg[:, cols], ident[:], start=True, stop=False, is_transpose=True)
-                nc.tensor.matmul(pull[:, d, :], yp[:, cols], ident[:], start=False, stop=True, is_transpose=True)
+        def turn(dst, src, start, stop):
+            nc.tensor.matmul(dst, src, ident[:], start=start, stop=stop, is_transpose=True)
 
-        def clip_and_turn_back(k):
-            v0, pulls = UNITS[k][1], centres[k][2]
-            total = bank(UNITS[k][4], [P, len(pulls) * P])
-            for c, pull in enumerate(pulls):
-                chunk = v0 // P + c
-                clipped = work(k, "clipped%d" % c, [P, NEIGHBOURS, P])
-                if k == last:
-                    nc.vector.tensor_scalar(
-                        clipped[:], pull[:], hi[:, chunk : chunk + 1], lo[:, chunk : chunk + 1], ALU.min, ALU.max
-                    )
-                else:
-                    staged = work(k, "staged%d" % c, [P, NEIGHBOURS, P])
-                    nc.scalar.copy(staged[:], pull[:])
-                    nc.gpsimd.tensor_scalar(
-                        clipped[:], staged[:], hi[:, chunk : chunk + 1], lo[:, chunk : chunk + 1], ALU.min, ALU.max
-                    )
-                for d in range(NEIGHBOURS):
-                    nc.tensor.matmul(
-                        total[:, c * P : (c + 1) * P],
-                        clipped[:, d, :],
-                        ident[:],
-                        start=(d == 0),
-                        stop=(d == NEIGHBOURS - 1),
-                        is_transpose=True,
-                    )
-            return total
-
-        def finish(k):
-            b, v0, width = UNITS[k][:3]
-            result = work(k, "result", [P, width])
-            nc.vector.scalar_tensor_tensor(result[:], summed[k][:], 1.0 / NEIGHBOURS, centres[k][0][:], ALU.mult, ALU.add)
-            nc.sync.dma_start(out[b * P : (b + 1) * P, v0 : v0 + width], result[:])
-
-        centres, summed = {}, {}
-        for k in range(len(UNITS)):
-            centres[k] = gather_centres(k)
+        def form_pulls(k):
+            b, c = divmod(k, V // P)
+            neg = negs[b][:, c * P : (c + 1) * P]
+            pull = bank(PULL_BANKS[k % len(PULL_BANKS)], [P, NEIGHBOURS, P])
             for d in range(NEIGHBOURS):
-                tag = None
-                if d == 0 and k >= 2:
-                    finish(k - 2)
-                if d == 0 and k >= 1:
-                    summed[k - 1] = clip_and_turn_back(k - 1)
-                    pass
-                gather_neighbours(k, d, tag)
-        finish(last - 1)
-        summed[last] = clip_and_turn_back(last)
-        finish(last)
+                turn(pull[:, d, :], neg, d == 0, False)
+            yp = work(k, "yp", [P, NEIGHBOURS, P], "staged%d" % (k - LAG))
+            for d in range(NEIGHBOURS):
+                nc.vector.tensor_copy(yp[:, d, :], y[b][:, 0:S].indirect(entries(pos_sb[d], c * P, P)))
+                turn(pull[:, d, :], yp[:, d, :], False, d == NEIGHBOURS - 1)
+            return pull
+
+        def clip(k):
+            c = k % (V // P)
+            src = pulls[k]
+            if k < CHUNKS - DIRECT:
+                src = work(k, "staged", [P, NEIGHBOURS, P])
+                nc.scalar.copy(src[:], pulls[k][:])
+            clipped = work(k, "clipped", [P, NEIGHBOURS, P])
+            nc.vector.tensor_scalar(clipped[:], src[:], hi[:, c : c + 1], lo[:, c : c + 1], ALU.min, ALU.max)
+            return clipped
+
+        def finish(first, count, bank_index, tag):
+            b, c0 = divmod(first, V // P)
+            cols = slice(c0 * P, (c0 + count) * P)
+            total = bank(bank_index, [P, count * P])
+            for c in range(count):
+                for d in range(NEIGHBOURS):
+                    turn(total[:, c * P : (c + 1) * P], clips[first + c][:, d, :], d == 0, d == NEIGHBOURS - 1)
+            result = work(first, "result", [P, count * P], tag)
+            nc.vector.scalar_tensor_tensor(result[:], total[:], 1.0 / NEIGHBOURS, negs[b][:, cols], ALU.mult, ALU.subtract)
+            nc.sync.dma_start(out[b * P : (b + 1) * P, cols], result[:])
+
+        negs, pulls, clips = {}, {}, {}
+        for k in range(CHUNKS + LAG + 1):
+            if LAG <= k < CHUNKS + LAG:
+                clips[k - LAG] = clip(k - LAG)
+            if k < CHUNKS:
+                if k % (V // P) == 0:
+                    negs[k // (V // P)] = gather_centres(k // (V // P))
+                pulls[k] = form_pulls(k)
+            for job in FINISHES:
+                if job[0] + job[1] - 1 == k - LAG - 1 + 1:
+                    finish(*job)

@@ -23,9 +23,10 @@ LANES = 16
 NEIGHBOURS = 3
 CHUNKS = BLOCKS * V // P
 PULL_BANKS = (6, 7, 0, 1)
-LAG = 3
+GATHERS = [(0, 2, None), (2, 2, "w_bf11"), (4, 1, None), (5, 1, None), (6, 1, None), (7, 1, None)]
 DIRECT = 2
-FINISHES = [(0, 2, 2, "staged1"), (2, 2, 3, "staged3"), (4, 2, 4, None), (6, 1, 5, None), (7, 1, 2, None)]
+LAG = 2
+FINISHES = [(0, 2, 2, None), (2, 2, 3, "lo"), (4, 2, 4, None), (6, 1, 5, None), (7, 1, 2, None)]
 
 
 def tile_picked_huber_none_p_kernel(
@@ -71,7 +72,7 @@ def tile_picked_huber_none_p_kernel(
         hi = keep.tile([P, V // P], F32, name="hi")
         with nc.allow_non_contiguous_dma(reason="one bound a partition"):
             nc.sync.dma_start(hi[:], bound[0, :].rearrange("(c p) -> p c", p=P))
-        lo = keep.tile([P, V // P], F32, name="lo")
+        lo = keep.tile([P, V // P], F32, name="lo", tag="lo", align_bytes=64)
         nc.scalar.mul(lo[:], hi[:], -1.0)
 
         ident = keep.tile([P, P], F32, name="ident")
@@ -94,10 +95,17 @@ def tile_picked_huber_none_p_kernel(
 
         def quantise_weights(z, b):
             grouped = keep.tile([P, P, PACK], BF16, name="w_bf", tag="w_bf%d%d" % (z, b), align_bytes=64)
-            nc.scalar.copy(
-                grouped[:].rearrange("p (c i) j -> p c j i", i=4),
-                w_raw[z, b].rearrange("p j (c i) -> p c j i", i=4),
-            )
+            dst = grouped[:].rearrange("p (c i) j -> p c j i", i=4)
+            src = w_raw[z, b].rearrange("p j (c i) -> p c j i", i=4)
+            if b == 1:
+                nc.gpsimd.tensor_scalar(
+                    grouped[:], w_raw[z, b].rearrange("p j c -> p c j"), 1.0, 0.0, ALU.mult, ALU.add
+                )
+            elif z == 0:
+                nc.scalar.copy(dst, src)
+            else:
+                nc.scalar.copy(dst[:, 0:16], src[:, 0:16])
+                nc.vector.tensor_copy(dst[:, 16:32], src[:, 16:32])
             w_codes[z, b] = keep.tile([P, P], U32, name="w_codes%d%d" % (z, b), align_bytes=64)
             w_sc[z, b] = keep.tile([P, P], U8, name="w_sc%d%d" % (z, b), align_bytes=64)
             nc.vector.quantize_mx(
@@ -123,7 +131,10 @@ def tile_picked_huber_none_p_kernel(
                     start=(z == 0),
                     stop=(z == PASSES - 1),
                 )
-            nc.scalar.copy(y[b][:, cols], acc[:])
+            if b == 0 and start + count == S:
+                nc.vector.tensor_copy(y[b][:, cols], acc[:])
+            else:
+                nc.scalar.copy(y[b][:, cols], acc[:])
 
         first = gather_words(0, 0, S, "x_first")
         for start, count in pieces:
@@ -141,7 +152,7 @@ def tile_picked_huber_none_p_kernel(
             project(1, piece, 3 + i)
 
         def work(k, role, shape, tag=None):
-            return keep.tile(shape, F32, name=role, tag=tag or "%s%d" % (role, k))
+            return keep.tile(shape, F32, name=role, tag=tag or "%s%d" % (role, k), align_bytes=64)
 
         def gather_centres(b):
             neg = work(b, "neg", [P, V])
@@ -151,47 +162,64 @@ def tile_picked_huber_none_p_kernel(
         def turn(dst, src, start, stop):
             nc.tensor.matmul(dst, src, ident[:], start=start, stop=stop, is_transpose=True)
 
-        def form_pulls(k):
-            b, c = divmod(k, V // P)
-            neg = negs[b][:, c * P : (c + 1) * P]
-            pull = bank(PULL_BANKS[k % len(PULL_BANKS)], [P, NEIGHBOURS, P])
+        def form_pulls(first, count, tag):
+            b, c0 = divmod(first, V // P)
+            for k in range(first, first + count):
+                c = k % (V // P)
+                pulls[k] = bank(PULL_BANKS[k % len(PULL_BANKS)], [P, NEIGHBOURS, P])
+                for d in range(NEIGHBOURS):
+                    turn(pulls[k][:, d, :], negs[b][:, c * P : (c + 1) * P], d == 0, False)
+            yp = work(first, "yp", [P, NEIGHBOURS, count * P], tag)
             for d in range(NEIGHBOURS):
-                turn(pull[:, d, :], neg, d == 0, False)
-            yp = work(k, "yp", [P, NEIGHBOURS, P], "staged%d" % (k - LAG))
-            for d in range(NEIGHBOURS):
-                nc.vector.tensor_copy(yp[:, d, :], y[b][:, 0:S].indirect(entries(pos_sb[d], c * P, P)))
-                turn(pull[:, d, :], yp[:, d, :], False, d == NEIGHBOURS - 1)
-            return pull
+                nc.vector.tensor_copy(yp[:, d, :], y[b][:, 0:S].indirect(entries(pos_sb[d], c0 * P, count * P)))
+                for i in range(count):
+                    turn(pulls[first + i][:, d, :], yp[:, d, i * P : (i + 1) * P], False, d == NEIGHBOURS - 1)
 
-        def clip(k):
+        def clip_and_turn_back(k):
             c = k % (V // P)
-            src = pulls[k]
-            if k < CHUNKS - DIRECT:
-                src = work(k, "staged", [P, NEIGHBOURS, P])
-                nc.scalar.copy(src[:], pulls[k][:])
             clipped = work(k, "clipped", [P, NEIGHBOURS, P])
-            nc.vector.tensor_scalar(clipped[:], src[:], hi[:, c : c + 1], lo[:, c : c + 1], ALU.min, ALU.max)
-            return clipped
+            if k < CHUNKS - DIRECT:
+                staged = work(k, "staged", [P, NEIGHBOURS, P])
+                nc.scalar.copy(staged[:], pulls[k][:])
+                nc.gpsimd.tensor_scalar(clipped[:], staged[:], hi[:, c : c + 1], lo[:, c : c + 1], ALU.min, ALU.max)
+            else:
+                nc.vector.tensor_scalar(clipped[:], pulls[k][:], hi[:, c : c + 1], lo[:, c : c + 1], ALU.min, ALU.max)
+            for first, count, bank_index, tag in FINISHES:
+                if first == k:
+                    totals[first] = bank(bank_index, [P, count * P])
+                if first <= k < first + count:
+                    i = k - first
+                    for d in range(NEIGHBOURS):
+                        turn(totals[first][:, i * P : (i + 1) * P], clipped[:, d, :], d == 0, d == NEIGHBOURS - 1)
 
         def finish(first, count, bank_index, tag):
             b, c0 = divmod(first, V // P)
             cols = slice(c0 * P, (c0 + count) * P)
-            total = bank(bank_index, [P, count * P])
-            for c in range(count):
-                for d in range(NEIGHBOURS):
-                    turn(total[:, c * P : (c + 1) * P], clips[first + c][:, d, :], d == 0, d == NEIGHBOURS - 1)
             result = work(first, "result", [P, count * P], tag)
-            nc.vector.scalar_tensor_tensor(result[:], total[:], 1.0 / NEIGHBOURS, negs[b][:, cols], ALU.mult, ALU.subtract)
-            nc.sync.dma_start(out[b * P : (b + 1) * P, cols], result[:])
+            if first == 0:
+                mean = work(first, "mean", [P, count * P])
+                nc.scalar.mul(mean[:], totals[first][:], 1.0 / NEIGHBOURS)
+                nc.gpsimd.tensor_tensor(result[:], mean[:], negs[b][:, cols], ALU.subtract)
+            else:
+                nc.vector.scalar_tensor_tensor(
+                    result[:], totals[first][:], 1.0 / NEIGHBOURS, negs[b][:, cols], ALU.mult, ALU.subtract
+                )
+            queue = nc.scalar if first == CHUNKS - 1 else nc.sync
+            queue.dma_start(out[b * P : (b + 1) * P, cols], result[:])
 
-        negs, pulls, clips = {}, {}, {}
-        for k in range(CHUNKS + LAG + 1):
-            if LAG <= k < CHUNKS + LAG:
-                clips[k - LAG] = clip(k - LAG)
-            if k < CHUNKS:
-                if k % (V // P) == 0:
-                    negs[k // (V // P)] = gather_centres(k // (V // P))
-                pulls[k] = form_pulls(k)
-            for job in FINISHES:
-                if job[0] + job[1] - 1 == k - LAG - 1 + 1:
-                    finish(*job)
+        negs, pulls, totals = {}, {}, {}
+        clipped_to = 0
+        for first, count, tag in GATHERS:
+            if first % (V // P) == 0:
+                negs[first // (V // P)] = gather_centres(first // (V // P))
+            form_pulls(first, count, tag)
+            for k in range(clipped_to, first + count - LAG):
+                clip_and_turn_back(k)
+            clipped_to = first + count - LAG
+            if first == 4:
+                finish(*FINISHES[0])
+        for k in range(clipped_to, CHUNKS - 1):
+            clip_and_turn_back(k)
+        clip_and_turn_back(CHUNKS - 1)
+        for job in FINISHES[1:]:
+            finish(*job)

@@ -23,10 +23,10 @@ LANES = 16
 NEIGHBOURS = 3
 CHUNKS = BLOCKS * V // P
 PULL_BANKS = (6, 7, 0, 1)
-GATHERS = [(0, 2, None), (2, 2, "w_bf11"), (4, 1, None), (5, 1, None), (6, 1, None), (7, 1, None)]
+GATHERS = [(0, 2, None), (2, 2, None), (4, 1, None), (5, 1, None), (6, 1, None), (7, 1, None)]
 DIRECT = 2
 LAG = 2
-FINISHES = [(0, 2, 2, None), (2, 2, 3, "lo"), (4, 2, 4, None), (6, 1, 5, None), (7, 1, 2, None)]
+FINISHES = [(0, 2, 2, None), (2, 2, 3, "staged5"), (4, 2, 4, None), (6, 1, 5, None), (7, 1, 2, None)]
 
 
 def tile_picked_huber_none_p_kernel(
@@ -35,6 +35,7 @@ def tile_picked_huber_none_p_kernel(
     nc = tc.nc
     with ExitStack() as ctx:
         keep = ctx.enter_context(tc.tile_pool(name="keep", bufs=1))
+        shared = ctx.enter_context(tc.tile_pool(name="shared", bufs=1))
         psum = ctx.enter_context(tc.psum_pool(name="psum", bufs=1))
 
         def load_list(name, src):
@@ -76,7 +77,8 @@ def tile_picked_huber_none_p_kernel(
         nc.scalar.mul(lo[:], hi[:], -1.0)
 
         ident = keep.tile([P, P], F32, name="ident")
-        make_identity(nc, ident[:])
+        nc.vector.memset(ident[:], 0.0)
+        make_identity(nc, ident[:], nomemset=True)
 
         def entries(tile, start, count):
             return tile[:, start // LANES : (start + count) // LANES]
@@ -86,70 +88,78 @@ def tile_picked_huber_none_p_kernel(
         pieces = [(0, 512), (512, 256), (768, 256)]
         x_codes = {}
 
-        def gather_words(z, start, count, tag):
-            codes = keep.tile([P, count], U32, name="x_codes", tag=tag, align_bytes=64)
+        def gather_words(z, start, count, codes):
             nc.vector.tensor_copy(codes[:], word_win[z][:].bitcast(U32).indirect(entries(offs_sb, start, count)))
-            return codes
+            return codes[:]
 
-        w_codes, w_sc = {}, {}
+        w_bf, w_codes, w_sc = {}, {}, {}
+
+        def cast_weights(z, b, grouped):
+            if (z, b) == (1, 1):
+                nc.gpsimd.tensor_scalar(grouped, w_raw[z, b].rearrange("p j c -> p c j"), 1.0, 0.0, ALU.mult, ALU.add)
+            else:
+                nc.scalar.copy(
+                    grouped.rearrange("p (c i) j -> p c j i", i=4), w_raw[z, b].rearrange("p j (c i) -> p c j i", i=4)
+                )
+            w_bf[z, b] = grouped
 
         def quantise_weights(z, b):
-            grouped = keep.tile([P, P, PACK], BF16, name="w_bf", tag="w_bf%d%d" % (z, b), align_bytes=64)
-            dst = grouped[:].rearrange("p (c i) j -> p c j i", i=4)
-            src = w_raw[z, b].rearrange("p j (c i) -> p c j i", i=4)
-            if b == 1:
-                nc.gpsimd.tensor_scalar(
-                    grouped[:], w_raw[z, b].rearrange("p j c -> p c j"), 1.0, 0.0, ALU.mult, ALU.add
-                )
-            elif z == 0:
-                nc.scalar.copy(dst, src)
-            else:
-                nc.scalar.copy(dst[:, 0:16], src[:, 0:16])
-                nc.vector.tensor_copy(dst[:, 16:32], src[:, 16:32])
+            grouped = w_bf[z, b]
             w_codes[z, b] = keep.tile([P, P], U32, name="w_codes%d%d" % (z, b), align_bytes=64)
             w_sc[z, b] = keep.tile([P, P], U8, name="w_sc%d%d" % (z, b), align_bytes=64)
             nc.vector.quantize_mx(
                 out=w_codes[z, b][:].bitcast(FP8X4),
                 scales=w_sc[z, b][:],
-                in_=grouped[:].rearrange("p c j -> p (c j)"),
+                in_=grouped.rearrange("p c j -> p (c j)"),
             )
 
         def bank(index, shape):
             return psum.tile(shape, F32, name="bank", tag="bank%d" % index)
 
-        def project(b, piece, bank_index):
-            start, count = piece
-            cols = slice(start, start + count)
-            acc = bank(bank_index, [P, count])
-            for z in range(PASSES):
-                nc.tensor.matmul_mx(
-                    out=acc[:],
-                    lhsT=w_codes[z, b][:].bitcast(FP8X4),
-                    lhsT_scale=w_sc[z, b][:],
-                    rhs=x_codes[z, start].bitcast(FP8X4),
-                    rhs_scale=x_sc[4 * z :, cols],
-                    start=(z == 0),
-                    stop=(z == PASSES - 1),
-                )
-            if b == 0 and start + count == S:
-                nc.vector.tensor_copy(y[b][:, cols], acc[:])
-            else:
-                nc.scalar.copy(y[b][:, cols], acc[:])
+        def project(b, group, bank_index, copy):
+            first_col = group[0][0]
+            width = sum(count for start, count in group)
+            acc = bank(bank_index, [P, width])
+            for start, count in group:
+                for z in range(PASSES):
+                    nc.tensor.matmul_mx(
+                        out=acc[:, start - first_col : start - first_col + count],
+                        lhsT=w_codes[z, b][:].bitcast(FP8X4),
+                        lhsT_scale=w_sc[z, b][:],
+                        rhs=x_codes[z, start][:, 0:count].bitcast(FP8X4),
+                        rhs_scale=x_sc[4 * z :, start : start + count],
+                        start=(z == 0),
+                        stop=(z == PASSES - 1),
+                    )
+            copy(y[b][:, first_col : first_col + width], acc[:])
 
-        first = gather_words(0, 0, S, "x_first")
-        for start, count in pieces:
-            x_codes[0, start] = first[:, start : start + count]
+        def plain(name, shape, dtype):
+            return keep.tile(shape, dtype, name=name, align_bytes=64)
+
+        first = gather_words(0, 0, S, plain("x_first", [P, S], U32))
+        cast_weights(0, 0, plain("w_bf00", [P, P, PACK], BF16)[:])
         quantise_weights(0, 0)
-        x_codes[1, 0] = gather_words(1, 0, 512, "x_second")[:]
+        second = gather_words(1, 0, 512, plain("x_second", [P, 512], U32))
+        third = gather_words(1, 512, 256, plain("x_third", [P, 256], U32))
+        wide = shared.tile([P, 2, P, PACK], BF16, name="w_bf10", align_bytes=64, offset=0)
+        cast_weights(1, 0, wide[:, 0])
         quantise_weights(1, 0)
-        x_codes[1, 512] = gather_words(1, 512, 256, "w_bf10")[:]
-        x_codes[1, 768] = gather_words(1, 768, 256, "x_last")[:]
-        for i, piece in enumerate(pieces):
-            project(0, piece, i)
+        cast_weights(0, 1, plain("w_bf01", [P, P, PACK], BF16)[:])
+        cast_weights(1, 1, shared.tile([P, P, PACK], BF16, name="w_bf11", align_bytes=64, offset=1024)[:])
+        last = gather_words(1, 768, 256, shared.tile([P, 256], U32, name="x_last", align_bytes=64, offset=0))
+        for start in range(0, S, P):
+            x_codes[0, start] = first[:, start:S]
+        x_codes[1, 0], x_codes[1, 256], x_codes[1, 512] = second, second[:, 256:512], third
+        x_codes[1, 768], x_codes[1, 896] = last, last[:, P : 2 * P]
         for z in range(PASSES):
             quantise_weights(z, 1)
-        for i, piece in enumerate(pieces):
-            project(1, piece, 3 + i)
+        project(0, [(0, 256)], 0, nc.scalar.copy)
+        project(0, [(256, 256)], 1, nc.scalar.copy)
+        project(0, [(512, 256)], 2, nc.scalar.copy)
+        project(0, [(768, P)], 5, nc.vector.tensor_copy)
+        project(0, [(896, P)], 6, nc.scalar.copy)
+        project(1, pieces[:1], 3, nc.scalar.copy)
+        project(1, pieces[1:], 4, nc.scalar.copy)
 
         def work(k, role, shape, tag=None):
             return keep.tile(shape, F32, name=role, tag=tag or "%s%d" % (role, k), align_bytes=64)
@@ -167,13 +177,19 @@ def tile_picked_huber_none_p_kernel(
             for k in range(first, first + count):
                 c = k % (V // P)
                 pulls[k] = bank(PULL_BANKS[k % len(PULL_BANKS)], [P, NEIGHBOURS, P])
+                slots[k] = [pulls[k][:, d, :] for d in range(NEIGHBOURS)]
+                opens, closes = [0], [NEIGHBOURS - 1]
+                if k == CHUNKS - 1:
+                    pulls[CHUNKS] = bank(PULL_BANKS[0], [P, P])
+                    slots[k][-1] = pulls[CHUNKS][:]
+                    opens, closes = [0, NEIGHBOURS - 1], [NEIGHBOURS - 2, NEIGHBOURS - 1]
                 for d in range(NEIGHBOURS):
-                    turn(pulls[k][:, d, :], negs[b][:, c * P : (c + 1) * P], d == 0, False)
+                    turn(slots[k][d], negs[b][:, c * P : (c + 1) * P], d in opens, False)
             yp = work(first, "yp", [P, NEIGHBOURS, count * P], tag)
             for d in range(NEIGHBOURS):
                 nc.vector.tensor_copy(yp[:, d, :], y[b][:, 0:S].indirect(entries(pos_sb[d], c0 * P, count * P)))
                 for i in range(count):
-                    turn(pulls[first + i][:, d, :], yp[:, d, i * P : (i + 1) * P], False, d == NEIGHBOURS - 1)
+                    turn(slots[first + i][d], yp[:, d, i * P : (i + 1) * P], False, d in closes)
 
         def clip_and_turn_back(k):
             c = k % (V // P)
@@ -182,8 +198,11 @@ def tile_picked_huber_none_p_kernel(
                 staged = work(k, "staged", [P, NEIGHBOURS, P])
                 nc.scalar.copy(staged[:], pulls[k][:])
                 nc.gpsimd.tensor_scalar(clipped[:], staged[:], hi[:, c : c + 1], lo[:, c : c + 1], ALU.min, ALU.max)
-            else:
+            elif k < CHUNKS - 1:
                 nc.vector.tensor_scalar(clipped[:], pulls[k][:], hi[:, c : c + 1], lo[:, c : c + 1], ALU.min, ALU.max)
+            else:
+                nc.vector.tensor_scalar(clipped[:, 0:2, :], pulls[k][:, 0:2, :], hi[:, c : c + 1], lo[:, c : c + 1], ALU.min, ALU.max)
+                nc.vector.tensor_scalar(clipped[:, 2, :], pulls[CHUNKS][:], hi[:, c : c + 1], lo[:, c : c + 1], ALU.min, ALU.max)
             for first, count, bank_index, tag in FINISHES:
                 if first == k:
                     totals[first] = bank(bank_index, [P, count * P])
@@ -196,7 +215,7 @@ def tile_picked_huber_none_p_kernel(
             b, c0 = divmod(first, V // P)
             cols = slice(c0 * P, (c0 + count) * P)
             result = work(first, "result", [P, count * P], tag)
-            if first == 0:
+            if b == 0:
                 mean = work(first, "mean", [P, count * P])
                 nc.scalar.mul(mean[:], totals[first][:], 1.0 / NEIGHBOURS)
                 nc.gpsimd.tensor_tensor(result[:], mean[:], negs[b][:, cols], ALU.subtract)
@@ -207,7 +226,7 @@ def tile_picked_huber_none_p_kernel(
             queue = nc.scalar if first == CHUNKS - 1 else nc.sync
             queue.dma_start(out[b * P : (b + 1) * P, cols], result[:])
 
-        negs, pulls, totals = {}, {}, {}
+        negs, pulls, slots, totals = {}, {}, {}, {}
         clipped_to = 0
         for first, count, tag in GATHERS:
             if first % (V // P) == 0:

@@ -14,6 +14,7 @@ U16 = mybir.dt.uint16
 U8 = mybir.dt.uint8
 FP8X4 = mybir.dt.float8_e4m3fn_x4
 ALU = mybir.AluOpType
+COPY = mybir.ActivationFunctionType.Copy
 
 P = 128
 PACK = 4
@@ -22,11 +23,6 @@ BLOCKS = N // P
 LANES = 16
 NEIGHBOURS = 3
 CHUNKS = BLOCKS * V // P
-PULL_BANKS = (6, 7, 0, 1)
-GATHERS = [(0, 2, None), (2, 2, None), (4, 1, None), (5, 1, None), (6, 1, None), (7, 1, None)]
-DIRECT = 2
-LAG = 2
-FINISHES = [(0, 2, 2, None), (2, 2, 3, "staged5"), (4, 2, 4, None), (6, 1, 5, None), (7, 1, 2, None)]
 
 
 def tile_picked_huber_none_p_kernel(
@@ -54,10 +50,10 @@ def tile_picked_huber_none_p_kernel(
                 x_scales[:, 4 * q : 4 * q + 4, :].bitcast(I32),
             )
         word_win, w_raw = [], {}
-        y = [keep.tile([P, 2 * S], F32, name="y%d" % b) for b in range(BLOCKS)]
+        y = [keep.tile([P, S], F32, name="y%d" % b) for b in range(BLOCKS)]
 
         def load_weights(z, b):
-            raw = y[b][:, S + z * PACK * P : S + (z + 1) * PACK * P].rearrange("p (j c) -> p j c", j=PACK)
+            raw = keep.tile([P, PACK, P], F32, name="w_raw%d%d" % (z, b))[:]
             rows = w1[z * P * PACK : (z + 1) * P * PACK, b * P : (b + 1) * P]
             nc.sync.dma_start(raw, rows.rearrange("(p j) c -> p j c", j=PACK))
             w_raw[z, b] = raw
@@ -73,6 +69,10 @@ def tile_picked_huber_none_p_kernel(
         hi = keep.tile([P, V // P], F32, name="hi")
         with nc.allow_non_contiguous_dma(reason="one bound a partition"):
             nc.sync.dma_start(hi[:], bound[0, :].rearrange("(c p) -> p c", p=P))
+        reach = keep.tile([P, P], F32, name="reach", align_bytes=64)
+        nc.sync.dma_start(reach[:], bound[:, V - P : V])
+        reach_third = keep.tile([P, P], F32, name="reach_third", align_bytes=64)
+        nc.gpsimd.tensor_scalar(reach_third[:], reach[:], 1.0 / NEIGHBOURS, 0.0, ALU.mult, ALU.add)
         lo = keep.tile([P, V // P], F32, name="lo", tag="lo", align_bytes=64)
         nc.scalar.mul(lo[:], hi[:], -1.0)
 
@@ -131,7 +131,9 @@ def tile_picked_huber_none_p_kernel(
                         start=(z == 0),
                         stop=(z == PASSES - 1),
                     )
-            copy(y[b][:, first_col : first_col + width], acc[:])
+            if copy is not None:
+                copy(y[b][:, first_col : first_col + width], acc[:])
+            return acc
 
         def plain(name, shape, dtype):
             return keep.tile(shape, dtype, name=name, align_bytes=64)
@@ -158,87 +160,167 @@ def tile_picked_huber_none_p_kernel(
         project(0, [(512, 256)], 2, nc.scalar.copy)
         project(0, [(768, P)], 5, nc.vector.tensor_copy)
         project(0, [(896, P)], 6, nc.scalar.copy)
-        project(1, pieces[:1], 3, nc.scalar.copy)
-        project(1, pieces[1:], 4, nc.scalar.copy)
+
 
         def work(k, role, shape, tag=None):
             return keep.tile(shape, F32, name=role, tag=tag or "%s%d" % (role, k), align_bytes=64)
 
-        def gather_centres(b):
-            neg = work(b, "neg", [P, V])
-            nc.vector.tensor_scalar(neg[:], y[b][:].indirect(cen_sb[:]), -1.0, 0.0, ALU.mult, ALU.add)
-            return neg
-
         def turn(dst, src, start, stop):
             nc.tensor.matmul(dst, src, ident[:], start=start, stop=stop, is_transpose=True)
 
-        def form_pulls(first, count, tag):
+        negs = [work(b, "neg", [P, V]) for b in range(BLOCKS)]
+        pulls, clipped, totals, near = {}, {}, {}, {}
+
+        def centre(first, count=1):
             b, c0 = divmod(first, V // P)
-            for k in range(first, first + count):
-                c = k % (V // P)
-                pulls[k] = bank(PULL_BANKS[k % len(PULL_BANKS)], [P, NEIGHBOURS, P])
-                slots[k] = [pulls[k][:, d, :] for d in range(NEIGHBOURS)]
-                opens, closes = [0], [NEIGHBOURS - 1]
-                if k == CHUNKS - 1:
-                    pulls[CHUNKS] = bank(PULL_BANKS[0], [P, P])
-                    slots[k][-1] = pulls[CHUNKS][:]
-                    opens, closes = [0, NEIGHBOURS - 1], [NEIGHBOURS - 2, NEIGHBOURS - 1]
-                for d in range(NEIGHBOURS):
-                    turn(slots[k][d], negs[b][:, c * P : (c + 1) * P], d in opens, False)
-            yp = work(first, "yp", [P, NEIGHBOURS, count * P], tag)
+            return negs[b][:, c0 * P : (c0 + count) * P]
+
+        def picked(first, count, offsets):
+            b, c0 = divmod(first, V // P)
+            return y[b][:].indirect(entries(offsets, c0 * P, count * P))
+
+        def gather_centres(first, count):
+            nc.scalar.activation(centre(first, count), picked(first, count, cen_sb), COPY, scale=-1.0)
+
+        def gather(first, count, how, tag=None):
+            dst = work(first, "near", [P, NEIGHBOURS, count * P], tag)
             for d in range(NEIGHBOURS):
-                nc.vector.tensor_copy(yp[:, d, :], y[b][:, 0:S].indirect(entries(pos_sb[d], c0 * P, count * P)))
-                for i in range(count):
-                    turn(slots[first + i][d], yp[:, d, i * P : (i + 1) * P], False, d in closes)
+                src = picked(first, count, pos_sb[d])
+                if how[d] == "v":
+                    nc.vector.tensor_copy(dst[:, d, :], src)
+                elif how[d] == "f":
+                    nc.vector.tensor_tensor(dst[:, d, :], src, centre(first, count), ALU.add)
+                else:
+                    nc.scalar.activation(dst[:, d, :], src, COPY)
+            for i in range(count):
+                near[first + i] = dst[:, :, i * P : (i + 1) * P]
 
-        def clip_and_turn_back(k):
+        def subtract(k):
+            diff = work(k, "diff", [P, NEIGHBOURS, P])
+            spread = centre(k).unsqueeze(1).to_broadcast([P, NEIGHBOURS, P])
+            nc.gpsimd.tensor_tensor(diff[:], near[k], spread, ALU.add)
+            near[k] = diff[:]
+
+        def turn_centres(k, bank_index):
+            pulls[k] = bank(bank_index, [P, NEIGHBOURS, P])
+            for d in range(NEIGHBOURS):
+                turn(pulls[k][:, d, :], centre(k), d == 0, False)
+
+        def turn_near(k, bank_index=None):
+            if bank_index is not None:
+                pulls[k] = bank(bank_index, [P, NEIGHBOURS, P])
+            for d in range(NEIGHBOURS):
+                turn(pulls[k][:, d, :], near[k][:, d, :], d == 0 and bank_index is not None, d == NEIGHBOURS - 1)
+
+        def turn_mixed(k, bank_index, plain_slots):
+            pulls[k] = bank(bank_index, [P, NEIGHBOURS, P])
+            terms = [(d, centre(k)) for d in plain_slots] + [(d, near[k][:, d, :]) for d in range(NEIGHBOURS)]
+            for i, (d, src) in enumerate(terms):
+                turn(pulls[k][:, d, :], src, i == 0, i == len(terms) - 1)
+
+        def clip(k):
             c = k % (V // P)
-            clipped = work(k, "clipped", [P, NEIGHBOURS, P])
-            if k < CHUNKS - DIRECT:
-                staged = work(k, "staged", [P, NEIGHBOURS, P])
-                nc.scalar.copy(staged[:], pulls[k][:])
-                nc.gpsimd.tensor_scalar(clipped[:], staged[:], hi[:, c : c + 1], lo[:, c : c + 1], ALU.min, ALU.max)
-            elif k < CHUNKS - 1:
-                nc.vector.tensor_scalar(clipped[:], pulls[k][:], hi[:, c : c + 1], lo[:, c : c + 1], ALU.min, ALU.max)
-            else:
-                nc.vector.tensor_scalar(clipped[:, 0:2, :], pulls[k][:, 0:2, :], hi[:, c : c + 1], lo[:, c : c + 1], ALU.min, ALU.max)
-                nc.vector.tensor_scalar(clipped[:, 2, :], pulls[CHUNKS][:], hi[:, c : c + 1], lo[:, c : c + 1], ALU.min, ALU.max)
-            for first, count, bank_index, tag in FINISHES:
-                if first == k:
-                    totals[first] = bank(bank_index, [P, count * P])
-                if first <= k < first + count:
-                    i = k - first
-                    for d in range(NEIGHBOURS):
-                        turn(totals[first][:, i * P : (i + 1) * P], clipped[:, d, :], d == 0, d == NEIGHBOURS - 1)
+            clipped[k] = work(k, "clipped", [P, NEIGHBOURS, P])
+            nc.vector.tensor_scalar(clipped[k][:], pulls[k][:], hi[:, c : c + 1], lo[:, c : c + 1], ALU.min, ALU.max)
 
-        def finish(first, count, bank_index, tag):
+        def stage_and_clip(k):
+            c = k % (V // P)
+            staged = work(k, "staged", [P, NEIGHBOURS, P])
+            nc.scalar.copy(staged[:], pulls[k][:])
+            clipped[k] = work(k, "clipped", [P, NEIGHBOURS, P])
+            nc.gpsimd.tensor_scalar(clipped[k][:], staged[:], hi[:, c : c + 1], lo[:, c : c + 1], ALU.min, ALU.max)
+
+        def turn_back(first, count, bank_index):
+            totals[first] = bank(bank_index, [P, count * P])
+            for i in range(count):
+                for d in range(NEIGHBOURS):
+                    dst = totals[first][:, i * P : (i + 1) * P]
+                    turn(dst, clipped[first + i][:, d, :], d == 0, d == NEIGHBOURS - 1)
+
+        def finish(first, count, on_vector=True, queue=nc.sync, tag=None):
             b, c0 = divmod(first, V // P)
-            cols = slice(c0 * P, (c0 + count) * P)
             result = work(first, "result", [P, count * P], tag)
-            if b == 0:
+            if on_vector:
+                nc.vector.scalar_tensor_tensor(
+                    result[:], totals[first][:], 1.0 / NEIGHBOURS, centre(first, count), ALU.mult, ALU.subtract
+                )
+            else:
                 mean = work(first, "mean", [P, count * P])
                 nc.scalar.mul(mean[:], totals[first][:], 1.0 / NEIGHBOURS)
-                nc.gpsimd.tensor_tensor(result[:], mean[:], negs[b][:, cols], ALU.subtract)
-            else:
-                nc.vector.scalar_tensor_tensor(
-                    result[:], totals[first][:], 1.0 / NEIGHBOURS, negs[b][:, cols], ALU.mult, ALU.subtract
-                )
-            queue = nc.scalar if first == CHUNKS - 1 else nc.sync
-            queue.dma_start(out[b * P : (b + 1) * P, cols], result[:])
+                nc.gpsimd.tensor_tensor(result[:], mean[:], centre(first, count), ALU.subtract)
+            queue.dma_start(out[b * P : (b + 1) * P, c0 * P : (c0 + count) * P], result[:])
 
-        negs, pulls, slots, totals = {}, {}, {}, {}
-        clipped_to = 0
-        for first, count, tag in GATHERS:
-            if first % (V // P) == 0:
-                negs[first // (V // P)] = gather_centres(first // (V // P))
-            form_pulls(first, count, tag)
-            for k in range(clipped_to, first + count - LAG):
-                clip_and_turn_back(k)
-            clipped_to = first + count - LAG
-            if first == 4:
-                finish(*FINISHES[0])
-        for k in range(clipped_to, CHUNKS - 1):
-            clip_and_turn_back(k)
-        clip_and_turn_back(CHUNKS - 1)
-        for job in FINISHES[1:]:
-            finish(*job)
+        def limits(k):
+            upper, lower = work(k, "upper", [P, P]), work(k, "lower", [P, P])
+            nc.vector.tensor_tensor(upper[:], reach[:], centre(k), ALU.subtract)
+            nc.vector.scalar_tensor_tensor(
+                lower[:], centre(k), -1.0 / NEIGHBOURS, reach_third[:], ALU.mult, ALU.subtract
+            )
+            return upper, lower
+
+        def clamp_in_place(k, upper, lower):
+            b, c = divmod(k, V // P)
+            capped = work(k, "capped", [P, NEIGHBOURS, P], "diff5")
+            thirds = work(k, "thirds", [P, NEIGHBOURS, P])
+            for d0, d1 in ((0, 2), (2, 3)):
+                shape = [P, d1 - d0, P]
+                nc.vector.tensor_tensor(
+                    capped[:, d0:d1, :], near[k][:, d0:d1, :], upper[:].unsqueeze(1).to_broadcast(shape), ALU.min
+                )
+                nc.vector.scalar_tensor_tensor(
+                    thirds[:, d0:d1, :],
+                    capped[:, d0:d1, :],
+                    1.0 / NEIGHBOURS,
+                    lower[:].unsqueeze(1).to_broadcast(shape),
+                    ALU.mult,
+                    ALU.max,
+                )
+            pair = work(k, "pair", [P, P])
+            nc.vector.tensor_tensor(pair[:], thirds[:, 0, :], thirds[:, 1, :], ALU.add)
+            result = work(k, "result", [P, P])
+            nc.vector.tensor_tensor(result[:], pair[:], thirds[:, 2, :], ALU.add)
+            nc.scalar.dma_start(out[b * P : (b + 1) * P, c * P : (c + 1) * P], result[:])
+
+        low_half = project(1, pieces[:1], 3, None)
+        high_half = project(1, pieces[1:], 4, None)
+        gather_centres(0, 1)
+        gather_centres(1, 1)
+        gather_centres(2, 2)
+        nc.scalar.copy(y[1][:, 0:512], low_half[:])
+        nc.scalar.copy(y[1][:, 512:S], high_half[:])
+        gather(0, 1, "vff")
+        turn_mixed(0, 7, [0])
+        gather(1, 1, "fff")
+        turn_near(1, 0)
+        clip(0)
+        gather(2, 2, "fff")
+        gather_centres(4, 2)
+        gather(4, 1, "sss")
+        subtract(4)
+        gather(5, 1, "sss")
+        subtract(5)
+        clip(1)
+        turn_back(0, 2, 5)
+        turn_near(2, 1)
+        turn_near(3, 2)
+        clip(2)
+        clip(3)
+        finish(0, 2)
+        turn_near(4, 4)
+        turn_back(2, 2, 3)
+        gather_centres(6, 2)
+        turn_centres(6, 7)
+        clip(4)
+        finish(2, 2)
+        last_limits = limits(7)
+        turn_near(5, 0)
+        gather(6, 1, "sss")
+        turn_near(6)
+        clip(5)
+        turn_back(4, 2, 1)
+        clip(6)
+        turn_back(6, 1, 2)
+        gather(7, 1, "sss")
+        finish(4, 2)
+        finish(6, 1)
+        clamp_in_place(7, *last_limits)

@@ -43,7 +43,10 @@ def tile_picked_huber_none_p_kernel(
         nc.vector.memset(scale_win[:].bitcast(I32), 0)
         offs_sb = load_list("offs_sb", offs)
         cen_sb = load_list("cen_sb", cen)
-        pos_sb = [load_list("pos%d_sb" % d, (pos1, pos2, pos3)[d]) for d in range(1)]
+        reach = keep.tile([P, P], F32, name="reach", align_bytes=64)
+        nc.sync.dma_start(reach[:], bound[:, V - P : V])
+        reach_third = keep.tile([P, P], F32, name="reach_third", align_bytes=64)
+        nc.gpsimd.tensor_scalar(reach_third[:], reach[:], 1.0 / NEIGHBOURS, 0.0, ALU.mult, ALU.add)
         for q in range(4):
             nc.sync.dma_start(
                 scale_win[32 * q : 32 * q + 4 * PASSES, :].bitcast(I32),
@@ -65,14 +68,10 @@ def tile_picked_huber_none_p_kernel(
             load_weights(z, 0)
         for z in range(PASSES):
             load_weights(z, 1)
-        pos_sb = pos_sb + [load_list("pos%d_sb" % d, (pos1, pos2, pos3)[d]) for d in range(1, 3)]
+        pos_sb = [load_list("pos%d_sb" % d, (pos1, pos2, pos3)[d]) for d in range(NEIGHBOURS)]
         hi = keep.tile([P, V // P], F32, name="hi")
         with nc.allow_non_contiguous_dma(reason="one bound a partition"):
             nc.sync.dma_start(hi[:], bound[0, :].rearrange("(c p) -> p c", p=P))
-        reach = keep.tile([P, P], F32, name="reach", align_bytes=64)
-        nc.sync.dma_start(reach[:], bound[:, V - P : V])
-        reach_third = keep.tile([P, P], F32, name="reach_third", align_bytes=64)
-        nc.gpsimd.tensor_scalar(reach_third[:], reach[:], 1.0 / NEIGHBOURS, 0.0, ALU.mult, ALU.add)
         lo = keep.tile([P, V // P], F32, name="lo", tag="lo", align_bytes=64)
         nc.scalar.mul(lo[:], hi[:], -1.0)
 

from contextlib import ExitStack

import concourse.mybir as mybir
from concourse.masks import make_identity

K, T, S, V, N = 1024, 2048, 1024, 512, 256
FLOPS = 2 * K * S * N

F32 = mybir.dt.float32
BF16 = mybir.dt.bfloat16
I32 = mybir.dt.int32
U32 = mybir.dt.uint32
U16 = mybir.dt.uint16
U8 = mybir.dt.uint8
FP8X4 = mybir.dt.float8_e4m3fn_x4
ALU = mybir.AluOpType
COPY = mybir.ActivationFunctionType.Copy

P = 128
PACK = 4
PASSES = K // (P * PACK)
BLOCKS = N // P
LANES = 16
NEIGHBOURS = 3
CHUNKS = BLOCKS * V // P


def tile_picked_huber_none_p_kernel(
    tc, x_words, x_scales, w1, bound, offs, cen, pos1, pos2, pos3, out
):
    nc = tc.nc
    with ExitStack() as ctx:
        keep = ctx.enter_context(tc.tile_pool(name="keep", bufs=1))
        shared = ctx.enter_context(tc.tile_pool(name="shared", bufs=1))
        psum = ctx.enter_context(tc.psum_pool(name="psum", bufs=1))

        def load_list(name, src):
            tile = keep.tile(list(src.shape), U16, name=name)
            nc.sync.dma_start(tile[:], src)
            return tile

        scale_win = keep.tile([P, T], U8, name="scale_win", align_bytes=64)
        nc.vector.memset(scale_win[:].bitcast(I32), 0)
        offs_sb = load_list("offs_sb", offs)
        cen_sb = load_list("cen_sb", cen)
        reach = keep.tile([P, P], F32, name="reach", align_bytes=64)
        nc.sync.dma_start(reach[:], bound[:, V - P : V])
        reach_third = keep.tile([P, P], F32, name="reach_third", align_bytes=64)
        nc.gpsimd.tensor_scalar(reach_third[:], reach[:], 1.0 / NEIGHBOURS, 0.0, ALU.mult, ALU.add)
        for q in range(4):
            nc.sync.dma_start(
                scale_win[32 * q : 32 * q + 4 * PASSES, :].bitcast(I32),
                x_scales[:, 4 * q : 4 * q + 4, :].bitcast(I32),
            )
        word_win, w_raw = [], {}
        y = [keep.tile([P, S], F32, name="y%d" % b) for b in range(BLOCKS)]

        def load_weights(z, b):
            raw = keep.tile([P, PACK, P], F32, name="w_raw%d%d" % (z, b))[:]
            rows = w1[z * P * PACK : (z + 1) * P * PACK, b * P : (b + 1) * P]
            nc.sync.dma_start(raw, rows.rearrange("(p j) c -> p j c", j=PACK))
            w_raw[z, b] = raw

        for z in range(PASSES):
            win = keep.tile([P, T], I32, name="word_win%d" % z, align_bytes=64)
            nc.sync.dma_start(win[:], x_words[z].rearrange("p n t -> p (n t)").bitcast(I32))
            word_win.append(win)
            load_weights(z, 0)
        for z in range(PASSES):
            load_weights(z, 1)
        pos_sb = [load_list("pos%d_sb" % d, (pos1, pos2, pos3)[d]) for d in range(NEIGHBOURS)]
        hi = keep.tile([P, V // P], F32, name="hi")
        with nc.allow_non_contiguous_dma(reason="one bound a partition"):
            nc.sync.dma_start(hi[:], bound[0, :].rearrange("(c p) -> p c", p=P))
        lo = keep.tile([P, V // P], F32, name="lo", tag="lo", align_bytes=64)
        nc.scalar.mul(lo[:], hi[:], -1.0)

        ident = keep.tile([P, P], F32, name="ident")
        nc.vector.memset(ident[:], 0.0)
        make_identity(nc, ident[:], nomemset=True)

        def entries(tile, start, count):
            return tile[:, start // LANES : (start + count) // LANES]

        x_sc = keep.tile([P, S], U8, name="x_sc", align_bytes=64)
        nc.vector.tensor_copy(x_sc[:], scale_win[:].indirect(offs_sb[:]))
        pieces = [(0, 512), (512, 256), (768, 256)]
        x_codes = {}

        def gather_words(z, start, count, codes):
            nc.vector.tensor_copy(codes[:], word_win[z][:].bitcast(U32).indirect(entries(offs_sb, start, count)))
            return codes[:]

        w_bf, w_codes, w_sc = {}, {}, {}

        def cast_weights(z, b, grouped):
            if (z, b) == (1, 1):
                nc.gpsimd.tensor_scalar(grouped, w_raw[z, b].rearrange("p j c -> p c j"), 1.0, 0.0, ALU.mult, ALU.add)
            else:
                nc.scalar.copy(
                    grouped.rearrange("p (c i) j -> p c j i", i=4), w_raw[z, b].rearrange("p j (c i) -> p c j i", i=4)
                )
            w_bf[z, b] = grouped

        def quantise_weights(z, b):
            grouped = w_bf[z, b]
            w_codes[z, b] = keep.tile([P, P], U32, name="w_codes%d%d" % (z, b), align_bytes=64)
            w_sc[z, b] = keep.tile([P, P], U8, name="w_sc%d%d" % (z, b), align_bytes=64)
            nc.vector.quantize_mx(
                out=w_codes[z, b][:].bitcast(FP8X4),
                scales=w_sc[z, b][:],
                in_=grouped.rearrange("p c j -> p (c j)"),
            )

        def bank(index, shape):
            return psum.tile(shape, F32, name="bank", tag="bank%d" % index)

        def project(b, group, bank_index, copy):
            first_col = group[0][0]
            width = sum(count for start, count in group)
            acc = bank(bank_index, [P, width])
            for start, count in group:
                for z in range(PASSES):
                    nc.tensor.matmul_mx(
                        out=acc[:, start - first_col : start - first_col + count],
                        lhsT=w_codes[z, b][:].bitcast(FP8X4),
                        lhsT_scale=w_sc[z, b][:],
                        rhs=x_codes[z, start][:, 0:count].bitcast(FP8X4),
                        rhs_scale=x_sc[4 * z :, start : start + count],
                        start=(z == 0),
                        stop=(z == PASSES - 1),
                    )
            if copy is not None:
                copy(y[b][:, first_col : first_col + width], acc[:])
            return acc

        def plain(name, shape, dtype):
            return keep.tile(shape, dtype, name=name, align_bytes=64)

        first = gather_words(0, 0, S, plain("x_first", [P, S], U32))
        cast_weights(0, 0, plain("w_bf00", [P, P, PACK], BF16)[:])
        quantise_weights(0, 0)
        second = gather_words(1, 0, 512, plain("x_second", [P, 512], U32))
        third = gather_words(1, 512, 256, plain("x_third", [P, 256], U32))
        wide = shared.tile([P, 2, P, PACK], BF16, name="w_bf10", align_bytes=64, offset=0)
        cast_weights(1, 0, wide[:, 0])
        quantise_weights(1, 0)
        cast_weights(0, 1, plain("w_bf01", [P, P, PACK], BF16)[:])
        cast_weights(1, 1, shared.tile([P, P, PACK], BF16, name="w_bf11", align_bytes=64, offset=1024)[:])
        last = gather_words(1, 768, 256, shared.tile([P, 256], U32, name="x_last", align_bytes=64, offset=0))
        for start in range(0, S, P):
            x_codes[0, start] = first[:, start:S]
        x_codes[1, 0], x_codes[1, 256], x_codes[1, 512] = second, second[:, 256:512], third
        x_codes[1, 768], x_codes[1, 896] = last, last[:, P : 2 * P]
        for z in range(PASSES):
            quantise_weights(z, 1)
        project(0, [(0, 256)], 0, nc.scalar.copy)
        project(0, [(256, 256)], 1, nc.scalar.copy)
        project(0, [(512, 256)], 2, nc.scalar.copy)
        project(0, [(768, P)], 5, nc.vector.tensor_copy)
        project(0, [(896, P)], 6, nc.scalar.copy)


        def work(k, role, shape, tag=None):
            return keep.tile(shape, F32, name=role, tag=tag or "%s%d" % (role, k), align_bytes=64)

        def turn(dst, src, start, stop):
            nc.tensor.matmul(dst, src, ident[:], start=start, stop=stop, is_transpose=True)

        negs = [work(b, "neg", [P, V]) for b in range(BLOCKS)]
        pulls, clipped, totals, near = {}, {}, {}, {}

        def centre(first, count=1):
            b, c0 = divmod(first, V // P)
            return negs[b][:, c0 * P : (c0 + count) * P]

        def picked(first, count, offsets):
            b, c0 = divmod(first, V // P)
            return y[b][:].indirect(entries(offsets, c0 * P, count * P))

        def gather_centres(first, count):
            nc.scalar.activation(centre(first, count), picked(first, count, cen_sb), COPY, scale=-1.0)

        def gather(first, count, how, tag=None):
            dst = work(first, "near", [P, NEIGHBOURS, count * P], tag)
            for d in range(NEIGHBOURS):
                src = picked(first, count, pos_sb[d])
                if how[d] == "v":
                    nc.vector.tensor_copy(dst[:, d, :], src)
                elif how[d] == "f":
                    nc.vector.tensor_tensor(dst[:, d, :], src, centre(first, count), ALU.add)
                else:
                    nc.scalar.activation(dst[:, d, :], src, COPY)
            for i in range(count):
                near[first + i] = dst[:, :, i * P : (i + 1) * P]

        def subtract(k):
            diff = work(k, "diff", [P, NEIGHBOURS, P])
            spread = centre(k).unsqueeze(1).to_broadcast([P, NEIGHBOURS, P])
            nc.gpsimd.tensor_tensor(diff[:], near[k], spread, ALU.add)
            near[k] = diff[:]

        def turn_centres(k, bank_index):
            pulls[k] = bank(bank_index, [P, NEIGHBOURS, P])
            for d in range(NEIGHBOURS):
                turn(pulls[k][:, d, :], centre(k), d == 0, False)

        def turn_near(k, bank_index=None):
            if bank_index is not None:
                pulls[k] = bank(bank_index, [P, NEIGHBOURS, P])
            for d in range(NEIGHBOURS):
                turn(pulls[k][:, d, :], near[k][:, d, :], d == 0 and bank_index is not None, d == NEIGHBOURS - 1)

        def turn_mixed(k, bank_index, plain_slots):
            pulls[k] = bank(bank_index, [P, NEIGHBOURS, P])
            terms = [(d, centre(k)) for d in plain_slots] + [(d, near[k][:, d, :]) for d in range(NEIGHBOURS)]
            for i, (d, src) in enumerate(terms):
                turn(pulls[k][:, d, :], src, i == 0, i == len(terms) - 1)

        def clip(k):
            c = k % (V // P)
            clipped[k] = work(k, "clipped", [P, NEIGHBOURS, P])
            nc.vector.tensor_scalar(clipped[k][:], pulls[k][:], hi[:, c : c + 1], lo[:, c : c + 1], ALU.min, ALU.max)

        def stage_and_clip(k):
            c = k % (V // P)
            staged = work(k, "staged", [P, NEIGHBOURS, P])
            nc.scalar.copy(staged[:], pulls[k][:])
            clipped[k] = work(k, "clipped", [P, NEIGHBOURS, P])
            nc.gpsimd.tensor_scalar(clipped[k][:], staged[:], hi[:, c : c + 1], lo[:, c : c + 1], ALU.min, ALU.max)

        def turn_back(first, count, bank_index):
            totals[first] = bank(bank_index, [P, count * P])
            for i in range(count):
                for d in range(NEIGHBOURS):
                    dst = totals[first][:, i * P : (i + 1) * P]
                    turn(dst, clipped[first + i][:, d, :], d == 0, d == NEIGHBOURS - 1)

        def finish(first, count, on_vector=True, queue=nc.sync, tag=None):
            b, c0 = divmod(first, V // P)
            result = work(first, "result", [P, count * P], tag)
            if on_vector:
                nc.vector.scalar_tensor_tensor(
                    result[:], totals[first][:], 1.0 / NEIGHBOURS, centre(first, count), ALU.mult, ALU.subtract
                )
            else:
                mean = work(first, "mean", [P, count * P])
                nc.scalar.mul(mean[:], totals[first][:], 1.0 / NEIGHBOURS)
                nc.gpsimd.tensor_tensor(result[:], mean[:], centre(first, count), ALU.subtract)
            queue.dma_start(out[b * P : (b + 1) * P, c0 * P : (c0 + count) * P], result[:])

        def limits(k):
            upper, lower = work(k, "upper", [P, P]), work(k, "lower", [P, P])
            nc.vector.tensor_tensor(upper[:], reach[:], centre(k), ALU.subtract)
            nc.vector.scalar_tensor_tensor(
                lower[:], centre(k), -1.0 / NEIGHBOURS, reach_third[:], ALU.mult, ALU.subtract
            )
            return upper, lower

        def clamp_in_place(k, upper, lower):
            b, c = divmod(k, V // P)
            capped = work(k, "capped", [P, NEIGHBOURS, P], "diff5")
            thirds = work(k, "thirds", [P, NEIGHBOURS, P])
            for d0, d1 in ((0, 2), (2, 3)):
                shape = [P, d1 - d0, P]
                nc.vector.tensor_tensor(
                    capped[:, d0:d1, :], near[k][:, d0:d1, :], upper[:].unsqueeze(1).to_broadcast(shape), ALU.min
                )
                nc.vector.scalar_tensor_tensor(
                    thirds[:, d0:d1, :],
                    capped[:, d0:d1, :],
                    1.0 / NEIGHBOURS,
                    lower[:].unsqueeze(1).to_broadcast(shape),
                    ALU.mult,
                    ALU.max,
                )
            pair = work(k, "pair", [P, P])
            nc.vector.tensor_tensor(pair[:], thirds[:, 0, :], thirds[:, 1, :], ALU.add)
            result = work(k, "result", [P, P])
            nc.vector.tensor_tensor(result[:], pair[:], thirds[:, 2, :], ALU.add)
            nc.scalar.dma_start(out[b * P : (b + 1) * P, c * P : (c + 1) * P], result[:])

        low_half = project(1, pieces[:1], 3, None)
        high_half = project(1, pieces[1:], 4, None)
        gather_centres(0, 1)
        gather_centres(1, 1)
        gather_centres(2, 2)
        nc.scalar.copy(y[1][:, 0:512], low_half[:])
        nc.scalar.copy(y[1][:, 512:S], high_half[:])
        gather(0, 1, "vff")
        turn_mixed(0, 7, [0])
        gather(1, 1, "fff")
        turn_near(1, 0)
        clip(0)
        gather(2, 2, "fff")
        gather_centres(4, 2)
        gather(4, 1, "sss")
        subtract(4)
        gather(5, 1, "sss")
        subtract(5)
        clip(1)
        turn_back(0, 2, 5)
        turn_near(2, 1)
        turn_near(3, 2)
        clip(2)
        clip(3)
        finish(0, 2)
        turn_near(4, 4)
        turn_back(2, 2, 3)
        gather_centres(6, 2)
        turn_centres(6, 7)
        clip(4)
        finish(2, 2)
        last_limits = limits(7)
        turn_near(5, 0)
        gather(6, 1, "sss")
        turn_near(6)
        clip(5)
        turn_back(4, 2, 1)
        clip(6)
        turn_back(6, 1, 2)
        gather(7, 1, "sss")
        finish(4, 2)
        finish(6, 1)
        clamp_in_place(7, *last_limits)
